import numpy as np
import ml_dtypes


def mxq(x, axis, fmt="e4m3"):
    dtype, down = {"e4m3": (ml_dtypes.float8_e4m3fn, 7), "e5m2": (ml_dtypes.float8_e5m2, 14)}[fmt]
    v = np.moveaxis(np.asarray(x, np.float32).astype(ml_dtypes.bfloat16).astype(np.float64), axis, -1)
    blocks = v.reshape(v.shape[:-1] + (-1, 32))
    amax = np.abs(blocks).max(-1, keepdims=True)
    byte = np.maximum(np.where(amax > 0, np.frexp(amax)[1] - 1 + 127, 0) - down, 1)
    scale = np.exp2(byte - 127.0)
    codes = (blocks / scale).astype(np.float32).astype(dtype).astype(np.float64)
    return np.moveaxis((codes * scale).reshape(v.shape), -1, axis)


WIDE = False


def mx_kscale(k, group=512):
    if not WIDE:
        return np.ones(k)
    levels = np.array([18, -18])
    if group != 512:
        return np.exp2(np.random.permutation(np.resize(levels, k // group))).repeat(group)
    if k % 512:
        return np.exp2(np.random.permutation(np.resize(levels, k // 32))).repeat(32)
    a = np.empty((k // 512, 16))
    for p in range(k // 512):
        a[p, :8] = np.random.permutation(np.resize(levels, 8))
        for g in range(8):
            far = levels[np.abs(levels - a[p, g]) >= 10]
            a[p, g + 8] = far[np.random.randint(len(far))]
    return np.exp2(a.ravel()).repeat(32)


def f64(x):
    return np.asarray(x).astype(np.float64)


def bf(x):
    return np.asarray(x, np.float32).astype(ml_dtypes.bfloat16)


def planes(Y):
    r, m = Y.shape
    b = f64(bf(Y)).reshape(r // 32, 32, m)
    amax = np.abs(b).max(1)
    byte = np.clip(np.where(amax > 0, np.frexp(amax)[1] - 1 + 127 - 7, 1), 1, 254)
    codes = (b * np.exp2(127.0 - byte)[:, None, :]).reshape(r, m).astype(np.float32).astype(ml_dtypes.float8_e4m3fn).view(np.uint8)
    words = codes.reshape(r // 512, 128, 4, m).transpose(0, 1, 3, 2)
    return np.ascontiguousarray(words), np.ascontiguousarray(byte.astype(np.uint8).reshape(r // 512, 16, m))


G, D, I, Q, E = 8, 128, 128, 128, 128


def sgn(shape):
    return np.random.uniform(0.5, 2.0, shape) * np.where(np.random.standard_normal(shape) < 0, -1.0, 1.0)


def setup_inputs():
    n = np.random.standard_normal
    s_d = mx_kscale(D, 0)
    s_i = mx_kscale(I, 0)
    return {
        "kT": (n((G, D, I)) / np.sqrt(D) / s_d[:, None]).astype(np.float32),
        "qT": (n((G, D, Q)) * s_d[:, None]).astype(np.float32),
        "dk": (np.exp(-np.random.uniform(0.0, 3.0, (G, I, Q))) * (np.arange(I)[:, None] <= np.arange(Q)[None])).astype(np.float32),
        "t": (sgn((G, I, 1)) * s_i[:, None]).astype(np.float32),
        "v": ((n((G, I, E))) / s_i[:, None]).astype(np.float32),
        "S": (n((G, D, E)) / np.sqrt(D) / s_d[:, None]).astype(np.float32),
        "dq": (np.random.uniform(0.05, 1.0, (G, Q, 1))).astype(np.float32),
    }


def reference(kT, qT, dk, t, v, S, dq):
    kTq = mxq(f64(kT), 1, "e4m3")
    qTq = mxq(f64(qT), 1, "e4m3")
    z = kTq.transpose(0, 2, 1) @ qTq
    p = z * f64(dk) * f64(t)
    pq = mxq(p, 1, "e4m3")
    vq = mxq(f64(v), 1, "e4m3")
    y = pq.transpose(0, 2, 1) @ vq
    Sq = mxq(f64(S), 1, "e4m3")
    ys = qTq.transpose(0, 2, 1) @ Sq
    o = y + f64(dq) * ys
    Y = o.reshape(G * Q, E)
    words, scales = planes(Y)
    return Y, words, scales

@@ -1,0 +1,178 @@
+from contextlib import ExitStack
+
+import concourse.mybir as mybir
+
+G, D, I, Q, E = 8, 128, 128, 128, 128
+FLOPS = 3 * 2 * G * 128 * 128 * 128
+
+F32 = mybir.dt.float32
+BF16 = mybir.dt.bfloat16
+U32 = mybir.dt.uint32
+I32 = mybir.dt.int32
+U8 = mybir.dt.uint8
+FP8X4 = mybir.dt.float8_e4m3fn_x4
+ALU = mybir.AluOpType
+ACT = mybir.ActivationFunctionType
+
+P = 128
+ROWS = 32
+PACK = 4
+SIDE = 4
+SETS = G // SIDE
+W = 128
+
+
+def tile_rows_pl_win_ssd_kernel(tc, kT, qT, dk, t, v, S, dq, out_0, out_1, out_2):
+    nc = tc.nc
+    with ExitStack() as ctx:
+        sb = ctx.enter_context(tc.tile_pool(name="sb", bufs=1))
+        ps = ctx.enter_context(tc.psum_pool(name="ps", bufs=1))
+        ctx.enter_context(tc.manual_schedule())
+
+        def tiles(name, shape, dtype):
+            return [sb.tile(shape, dtype, name="%s%d" % (name, s), align_bytes=64) for s in range(SETS)]
+
+        raw = {n: tiles(n + "_raw", [P, PACK, W], F32) for n in ("k", "q", "v", "S")}
+        dk_sb = tiles("dk_sb", [P, SIDE, W], F32)
+        grouped = {n: tiles(n + "_grp", [P, W, PACK], BF16) for n in ("k", "q", "v", "S", "p", "o")}
+        codes = {n: tiles(n + "_codes", [P, W], U32) for n in ("k", "q", "v", "S", "p", "o")}
+        scales = {n: tiles(n + "_scales", [P, W], U8) for n in ("k", "q", "v", "S", "p")}
+        o_scales = sb.tile([P, SETS, W], U8, name="o_scales", align_bytes=64)
+        scales["o"] = [o_scales[:, s, :] for s in range(SETS)]
+        p_nat = tiles("p_nat", [P, SIDE, W], BF16)
+        p_row = tiles("p_row", [P, PACK, W], BF16)
+        o_nat = tiles("o_nat", [P, SIDE, W], F32)
+        ob_nat = tiles("ob_nat", [P, SIDE, W], BF16)
+        o_row = tiles("o_row", [P, PACK, W], BF16)
+        ys_sb = tiles("ys_sb", [P, SIDE, W], F32)
+        stage = sb.tile([P, 2, G, ROWS], F32, name="stage", align_bytes=64)
+        cols = sb.tile([P, 2 * G * ROWS], F32, name="cols", align_bytes=64)
+        banks = [[ps.tile([P, 4, W], F32, name="bank%d_%d" % (s, c)) for c in range(SIDE)] for s in range(SETS)]
+
+        def load(queue, name, src, s):
+            rows = src.rearrange("g d w -> (g d) w")[s * P * PACK : (s + 1) * P * PACK, :]
+            queue.dma_start(out=raw[name][s][:], in_=rows.rearrange("(p j) w -> p j w", j=PACK))
+
+        def interleave(copy, dst, src):
+            copy(
+                out=dst[:].rearrange("p (c i) j -> p c j i", i=4),
+                in_=src[:].rearrange("p j (c i) -> p c j i", i=4),
+            )
+
+        def quantise(name, s):
+            nc.vector.quantize_mx(
+                out=codes[name][s][:].bitcast(FP8X4),
+                scales=scales[name][s][:, :],
+                in_=grouped[name][s][:].rearrange("p w j -> p (w j)"),
+            )
+
+        def product(slot, a, b, s):
+            for c in range(SIDE):
+                r = slice(c * ROWS, (c + 1) * ROWS)
+                nc.tensor.matmul_mx(
+                    out=banks[s][c][:, slot, :],
+                    lhsT=codes[a][s][r, :].bitcast(FP8X4),
+                    lhsT_scale=scales[a][s][r, :],
+                    rhs=codes[b][s][r, :].bitcast(FP8X4),
+                    rhs_scale=scales[b][s][r, :],
+                    start=True,
+                    stop=True,
+                )
+
+        def column(which, g):
+            j = (which * G + g) * ROWS
+            return cols[:, j : j + 1]
+
+        def weights(s):
+            for c in range(SIDE):
+                nc.vector.scalar_tensor_tensor(
+                    out=p_nat[s][:, c, :], in0=banks[s][c][:, 0, :], scalar=column(0, s * SIDE + c),
+                    in1=dk_sb[s][:, c, :], op0=ALU.mult, op1=ALU.mult,
+                )
+                nc.sync.dma_start(out=p_row[s][c * ROWS : (c + 1) * ROWS, :, :], in_=p_nat[s][:, c, :])
+
+        def state_part(s):
+            for c in range(SIDE):
+                nc.scalar.activation(
+                    out=ys_sb[s][:, c, :], in_=banks[s][c][:, 1, :], func=ACT.Copy, scale=column(1, s * SIDE + c)
+                )
+
+        def result(s, dst):
+            for c in range(SIDE):
+                nc.vector.tensor_tensor(out=dst[s][:, c, :], in0=banks[s][c][:, 2, :], in1=ys_sb[s][:, c, :], op=ALU.add)
+                if dst is ob_nat:
+                    nc.sync.dma_start(out=o_row[s][c * ROWS : (c + 1) * ROWS, :, :], in_=ob_nat[s][:, c, :])
+
+        def store_result(s):
+            rows = out_0[s * SIDE * Q : (s + 1) * SIDE * Q, :]
+            nc.scalar.dma_start(out=rows.rearrange("(c q) e -> q c e", c=SIDE), in_=o_nat[s][:])
+
+        def store_words(s):
+            nc.sync.dma_start(
+                out=out_1[s].rearrange("x e u -> x (e u)").bitcast(I32), in_=codes["o"][s][:].bitcast(I32)
+            )
+
+        vcopy = nc.vector.tensor_copy
+        scopy = nc.scalar.copy
+
+        for s in range(SETS):
+            load(nc.sync, "k", kT, s)
+            load(nc.sync, "q", qT, s)
+        for s in range(SETS):
+            nc.sync.dma_start(out=dk_sb[s][:], in_=dk[s * SIDE : (s + 1) * SIDE].rearrange("c i q -> i c q"))
+        nc.vector.memset(stage[:], 0.0)
+        for which, src in enumerate((t, dq)):
+            nc.scalar.dma_start(
+                out=stage[0:P:ROWS, which, :, :], in_=src.rearrange("g (a r) o -> a g (r o)", a=P // ROWS)
+            )
+
+        interleave(scopy, grouped["k"][0], raw["k"][0])
+        interleave(vcopy, grouped["q"][0], raw["q"][0])
+        quantise("k", 0)
+        quantise("q", 0)
+        product(0, "k", "q", 0)
+        nc.vector.transpose(out=cols[:], in_=stage[:].rearrange("p a g r -> p (a g r)"))
+        interleave(scopy, grouped["k"][1], raw["k"][1])
+        load(nc.scalar, "S", S, 0)
+        load(nc.scalar, "S", S, 1)
+        interleave(vcopy, grouped["q"][1], raw["q"][1])
+        quantise("k", 1)
+        quantise("q", 1)
+        product(0, "k", "q", 1)
+        weights(0)
+        load(nc.scalar, "v", v, 0)
+        load(nc.scalar, "v", v, 1)
+        weights(1)
+        for s in range(SETS):
+            interleave(scopy, grouped["S"][s], raw["S"][s])
+            quantise("S", s)
+            product(1, "q", "S", s)
+        interleave(vcopy, grouped["p"][0], p_row[0])
+        interleave(scopy, grouped["v"][0], raw["v"][0])
+        state_part(0)
+        quantise("p", 0)
+        quantise("v", 0)
+        product(2, "p", "v", 0)
+        interleave(vcopy, grouped["p"][1], p_row[1])
+        interleave(scopy, grouped["v"][1], raw["v"][1])
+        state_part(1)
+        result(0, ob_nat)
+        quantise("p", 1)
+        quantise("v", 1)
+        product(2, "p", "v", 1)
+        result(0, o_nat)
+        store_result(0)
+        result(1, ob_nat)
+        result(1, o_nat)
+        store_result(1)
+        for s in range(SETS):
+            interleave(vcopy, grouped["o"][s], o_row[s])
+            quantise("o", s)
+            store_words(s)
+        scale_rows = out_2.bitcast(I32)
+        for c in range(SIDE):
+            queue = nc.scalar if c % 2 == 0 else nc.sync
+            queue.dma_start(
+                out=scale_rows[:, 4 * c : 4 * c + 4, :].rearrange("s f e -> f s e"),
+                in_=o_scales[c * ROWS : c * ROWS + 4, :, :].bitcast(I32),
+            )

@@ -20,6 +20,7 @@ PACK = 4
 SIDE = 4
 SETS = G // SIDE
 W = 128
+ORDER = [0, 2, 1, 3]
 
 
 def tile_rows_pl_win_ssd_kernel(tc, kT, qT, dk, t, v, S, dq, out_0, out_1, out_2):
@@ -32,7 +33,7 @@ def tile_rows_pl_win_ssd_kernel(tc, kT, qT, dk, t, v, S, dq, out_0, out_1, out_2
         def tiles(name, shape, dtype):
             return [sb.tile(shape, dtype, name="%s%d" % (name, s), align_bytes=64) for s in range(SETS)]
 
-        raw = {n: tiles(n + "_raw", [P, PACK, W], F32) for n in ("k", "q", "v", "S")}
+        raw = {n: tiles(n + "_raw", [P, PACK, W], F32) for n in ("k", "q", "S", "v")}
         dk_sb = tiles("dk_sb", [P, SIDE, W], F32)
         grouped = {n: tiles(n + "_grp", [P, W, PACK], BF16) for n in ("k", "q", "v", "S", "p", "o")}
         codes = {n: tiles(n + "_codes", [P, W], U32) for n in ("k", "q", "v", "S", "p", "o")}
@@ -45,19 +46,26 @@ def tile_rows_pl_win_ssd_kernel(tc, kT, qT, dk, t, v, S, dq, out_0, out_1, out_2
         ob_nat = tiles("ob_nat", [P, SIDE, W], BF16)
         o_row = tiles("o_row", [P, PACK, W], BF16)
         ys_sb = tiles("ys_sb", [P, SIDE, W], F32)
-        stage = sb.tile([P, 2, G, ROWS], F32, name="stage", align_bytes=64)
-        cols = sb.tile([P, 2 * G * ROWS], F32, name="cols", align_bytes=64)
+        stage = sb.tile([P, ROWS], F32, name="stage", align_bytes=64)
+        cols = sb.tile([P, ROWS], F32, name="cols", align_bytes=64)
         banks = [[ps.tile([P, 4, W], F32, name="bank%d_%d" % (s, c)) for c in range(SIDE)] for s in range(SETS)]
 
         def load(queue, name, src, s):
             rows = src.rearrange("g d w -> (g d) w")[s * P * PACK : (s + 1) * P * PACK, :]
             queue.dma_start(out=raw[name][s][:], in_=rows.rearrange("(p j) w -> p j w", j=PACK))
 
-        def interleave(copy, dst, src):
+        def load_dk(queue, s):
+            queue.dma_start(out=dk_sb[s][:], in_=dk[s * SIDE : (s + 1) * SIDE].rearrange("c i q -> i c q"))
+
+        def interleave(copy, dst, src, lo=0, hi=W):
             copy(
-                out=dst[:].rearrange("p (c i) j -> p c j i", i=4),
-                in_=src[:].rearrange("p j (c i) -> p c j i", i=4),
+                out=dst[:, lo:hi, :].rearrange("p (c i) j -> p c j i", i=4),
+                in_=src[:, :, lo:hi].rearrange("p j (c i) -> p c j i", i=4),
             )
+
+        def shared(dst, src, cut):
+            interleave(nc.vector.tensor_copy, dst, src, 0, cut)
+            interleave(nc.scalar.copy, dst, src, cut, W)
 
         def quantise(name, s):
             nc.vector.quantize_mx(
@@ -80,11 +88,11 @@ def tile_rows_pl_win_ssd_kernel(tc, kT, qT, dk, t, v, S, dq, out_0, out_1, out_2
                 )
 
         def column(which, g):
-            j = (which * G + g) * ROWS
+            j = 4 * g + which
             return cols[:, j : j + 1]
 
-        def weights(s):
-            for c in range(SIDE):
+        def weights(s, order=range(SIDE)):
+            for c in order:
                 nc.vector.scalar_tensor_tensor(
                     out=p_nat[s][:, c, :], in0=banks[s][c][:, 0, :], scalar=column(0, s * SIDE + c),
                     in1=dk_sb[s][:, c, :], op0=ALU.mult, op1=ALU.mult,
@@ -97,82 +105,94 @@ def tile_rows_pl_win_ssd_kernel(tc, kT, qT, dk, t, v, S, dq, out_0, out_1, out_2
                     out=ys_sb[s][:, c, :], in_=banks[s][c][:, 1, :], func=ACT.Copy, scale=column(1, s * SIDE + c)
                 )
 
-        def result(s, dst):
-            for c in range(SIDE):
-                nc.vector.tensor_tensor(out=dst[s][:, c, :], in0=banks[s][c][:, 2, :], in1=ys_sb[s][:, c, :], op=ALU.add)
-                if dst is ob_nat:
-                    nc.sync.dma_start(out=o_row[s][c * ROWS : (c + 1) * ROWS, :, :], in_=ob_nat[s][:, c, :])
+        def regroup_result(s, c, queue):
+            queue.dma_start(out=o_row[s][c * ROWS : (c + 1) * ROWS, :, :], in_=ob_nat[s][:, c, :])
 
-        def store_result(s):
-            rows = out_0[s * SIDE * Q : (s + 1) * SIDE * Q, :]
-            nc.scalar.dma_start(out=rows.rearrange("(c q) e -> q c e", c=SIDE), in_=o_nat[s][:])
+        def result(s, dst, order=range(SIDE)):
+            for c in order:
+                nc.vector.tensor_tensor(
+                    out=dst[s][:, c, :], in0=banks[s][c][:, 2, :], in1=ys_sb[s][:, c, :], op=ALU.add
+                )
+                if dst is ob_nat:
+                    regroup_result(s, c, nc.sync)
+
+        def store_result(s, queue=nc.scalar, lo=0, hi=SIDE):
+            rows = out_0[(s * SIDE + lo) * Q : (s * SIDE + hi) * Q, :]
+            queue.dma_start(out=rows.rearrange("(c q) e -> q c e", q=Q), in_=o_nat[s][:, lo:hi, :])
 
         def store_words(s):
             nc.sync.dma_start(
                 out=out_1[s].rearrange("x e u -> x (e u)").bitcast(I32), in_=codes["o"][s][:].bitcast(I32)
             )
 
+        def store_scales():
+            scale_rows = out_2.bitcast(I32)
+            for c in range(SIDE):
+                queue = nc.scalar if c % 2 == 0 else nc.sync
+                queue.dma_start(
+                    out=scale_rows[:, 4 * c : 4 * c + 4, :].rearrange("s f e -> f s e"),
+                    in_=o_scales[c * ROWS : c * ROWS + 4, :, :].bitcast(I32),
+                )
+
         vcopy = nc.vector.tensor_copy
         scopy = nc.scalar.copy
 
+        nc.vector.memset(stage[:], 0.0)
         for s in range(SETS):
             load(nc.sync, "k", kT, s)
             load(nc.sync, "q", qT, s)
-        for s in range(SETS):
-            nc.sync.dma_start(out=dk_sb[s][:], in_=dk[s * SIDE : (s + 1) * SIDE].rearrange("c i q -> i c q"))
-        nc.vector.memset(stage[:], 0.0)
         for which, src in enumerate((t, dq)):
-            nc.scalar.dma_start(
-                out=stage[0:P:ROWS, which, :, :], in_=src.rearrange("g (a r) o -> a g (r o)", a=P // ROWS)
-            )
+            nc.scalar.dma_start(out=stage[which:P:4, :], in_=src.rearrange("g (a r) o -> a g (r o)", a=P // ROWS))
+        for s in range(SETS):
+            load_dk(nc.sync, s)
+        load(nc.sync, "S", S, 0)
+        load(nc.sync, "S", S, 1)
 
         interleave(scopy, grouped["k"][0], raw["k"][0])
         interleave(vcopy, grouped["q"][0], raw["q"][0])
         quantise("k", 0)
         quantise("q", 0)
         product(0, "k", "q", 0)
-        nc.vector.transpose(out=cols[:], in_=stage[:].rearrange("p a g r -> p (a g r)"))
+        nc.vector.transpose(out=cols[:], in_=stage[:])
         interleave(scopy, grouped["k"][1], raw["k"][1])
-        load(nc.scalar, "S", S, 0)
-        load(nc.scalar, "S", S, 1)
         interleave(vcopy, grouped["q"][1], raw["q"][1])
         quantise("k", 1)
         quantise("q", 1)
         product(0, "k", "q", 1)
-        weights(0)
-        load(nc.scalar, "v", v, 0)
-        load(nc.scalar, "v", v, 1)
-        weights(1)
+        weights(0, ORDER)
+        load(nc.sync, "v", v, 0)
+        weights(1, ORDER)
+        load(nc.sync, "v", v, 1)
+        interleave(vcopy, grouped["S"][0], raw["S"][0])
+        interleave(scopy, grouped["S"][1], raw["S"][1])
         for s in range(SETS):
-            interleave(scopy, grouped["S"][s], raw["S"][s])
             quantise("S", s)
             product(1, "q", "S", s)
+            state_part(s)
         interleave(vcopy, grouped["p"][0], p_row[0])
-        interleave(scopy, grouped["v"][0], raw["v"][0])
-        state_part(0)
+        interleave(vcopy, grouped["v"][0], raw["v"][0])
         quantise("p", 0)
         quantise("v", 0)
         product(2, "p", "v", 0)
         interleave(vcopy, grouped["p"][1], p_row[1])
-        interleave(scopy, grouped["v"][1], raw["v"][1])
-        state_part(1)
-        result(0, ob_nat)
         quantise("p", 1)
+        shared(grouped["v"][1], raw["v"][1], 64)
+        result(0, ob_nat, ORDER[:1])
         quantise("v", 1)
         product(2, "p", "v", 1)
-        result(0, o_nat)
-        store_result(0)
-        result(1, ob_nat)
-        result(1, o_nat)
-        store_result(1)
+        result(0, ob_nat, ORDER[1:])
+        result(1, ob_nat, ORDER)
+        result(0, o_nat, range(0, 2))
+        store_result(0, nc.sync, 0, 2)
+        result(0, o_nat, range(2, 4))
+        store_result(0, nc.sync, 2, 4)
+        interleave(scopy, grouped["o"][0], o_row[0])
+        result(1, o_nat, range(0, 2))
+        store_result(1, nc.sync, 0, 2)
+        result(1, o_nat, range(2, 4))
+        store_result(1, nc.sync, 2, 4)
+        shared(grouped["o"][1], o_row[1], 88)
         for s in range(SETS):
-            interleave(vcopy, grouped["o"][s], o_row[s])
             quantise("o", s)
             store_words(s)
-        scale_rows = out_2.bitcast(I32)
-        for c in range(SIDE):
-            queue = nc.scalar if c % 2 == 0 else nc.sync
-            queue.dma_start(
-                out=scale_rows[:, 4 * c : 4 * c + 4, :].rearrange("s f e -> f s e"),
-                in_=o_scales[c * ROWS : c * ROWS + 4, :, :].bitcast(I32),
-            )
+        store_scales()

@@ -114,7 +114,7 @@ def tile_rows_pl_win_ssd_kernel(tc, kT, qT, dk, t, v, S, dq, out_0, out_1, out_2
                     out=dst[s][:, c, :], in0=banks[s][c][:, 2, :], in1=ys_sb[s][:, c, :], op=ALU.add
                 )
                 if dst is ob_nat:
-                    regroup_result(s, c, nc.sync)
+                    regroup_result(s, c, nc.sync if c < 2 else nc.scalar)
 
         def store_result(s, queue=nc.scalar, lo=0, hi=SIDE):
             rows = out_0[(s * SIDE + lo) * Q : (s * SIDE + hi) * Q, :]
@@ -138,15 +138,17 @@ def tile_rows_pl_win_ssd_kernel(tc, kT, qT, dk, t, v, S, dq, out_0, out_1, out_2
         scopy = nc.scalar.copy
 
         nc.vector.memset(stage[:], 0.0)
-        for s in range(SETS):
-            load(nc.sync, "k", kT, s)
-            load(nc.sync, "q", qT, s)
+        load(nc.sync, "k", kT, 0)
+        load(nc.sync, "q", qT, 0)
         for which, src in enumerate((t, dq)):
-            nc.scalar.dma_start(out=stage[which:P:4, :], in_=src.rearrange("g (a r) o -> a g (r o)", a=P // ROWS))
+            nc.sync.dma_start(out=stage[which:P:4, :], in_=src.rearrange("g (a r) o -> a g (r o)", a=P // ROWS))
+        load(nc.sync, "k", kT, 1)
+        load(nc.sync, "q", qT, 1)
         for s in range(SETS):
             load_dk(nc.sync, s)
         load(nc.sync, "S", S, 0)
         load(nc.sync, "S", S, 1)
+        load(nc.sync, "v", v, 0)
 
         interleave(scopy, grouped["k"][0], raw["k"][0])
         interleave(vcopy, grouped["q"][0], raw["q"][0])
@@ -160,37 +162,34 @@ def tile_rows_pl_win_ssd_kernel(tc, kT, qT, dk, t, v, S, dq, out_0, out_1, out_2
         quantise("q", 1)
         product(0, "k", "q", 1)
         weights(0, ORDER)
-        load(nc.sync, "v", v, 0)
-        weights(1, ORDER)
         load(nc.sync, "v", v, 1)
+        weights(1, ORDER)
         interleave(vcopy, grouped["S"][0], raw["S"][0])
         interleave(scopy, grouped["S"][1], raw["S"][1])
-        for s in range(SETS):
-            quantise("S", s)
-            product(1, "q", "S", s)
-            state_part(s)
-        interleave(vcopy, grouped["p"][0], p_row[0])
+        quantise("S", 0)
+        product(1, "q", "S", 0)
+        state_part(0)
         interleave(vcopy, grouped["v"][0], raw["v"][0])
-        quantise("p", 0)
+        quantise("S", 1)
+        product(1, "q", "S", 1)
+        state_part(1)
         quantise("v", 0)
+        interleave(vcopy, grouped["p"][0], p_row[0])
+        quantise("p", 0)
         product(2, "p", "v", 0)
+        interleave(vcopy, grouped["v"][1], raw["v"][1])
         interleave(vcopy, grouped["p"][1], p_row[1])
-        quantise("p", 1)
-        shared(grouped["v"][1], raw["v"][1], 64)
-        result(0, ob_nat, ORDER[:1])
         quantise("v", 1)
+        quantise("p", 1)
         product(2, "p", "v", 1)
+        result(0, ob_nat, ORDER[:1])
         result(0, ob_nat, ORDER[1:])
         result(1, ob_nat, ORDER)
-        result(0, o_nat, range(0, 2))
-        store_result(0, nc.sync, 0, 2)
-        result(0, o_nat, range(2, 4))
-        store_result(0, nc.sync, 2, 4)
+        result(0, o_nat, ORDER)
+        store_result(0, nc.sync)
         interleave(scopy, grouped["o"][0], o_row[0])
-        result(1, o_nat, range(0, 2))
-        store_result(1, nc.sync, 0, 2)
-        result(1, o_nat, range(2, 4))
-        store_result(1, nc.sync, 2, 4)
+        result(1, o_nat, ORDER)
+        store_result(1, nc.sync)
         shared(grouped["o"][1], o_row[1], 88)
         for s in range(SETS):
             quantise("o", s)

from contextlib import ExitStack

import concourse.mybir as mybir

G, D, I, Q, E = 8, 128, 128, 128, 128
FLOPS = 3 * 2 * G * 128 * 128 * 128

F32 = mybir.dt.float32
BF16 = mybir.dt.bfloat16
U32 = mybir.dt.uint32
I32 = mybir.dt.int32
U8 = mybir.dt.uint8
FP8X4 = mybir.dt.float8_e4m3fn_x4
ALU = mybir.AluOpType
ACT = mybir.ActivationFunctionType

P = 128
ROWS = 32
PACK = 4
SIDE = 4
SETS = G // SIDE
W = 128
ORDER = [0, 2, 1, 3]


def tile_rows_pl_win_ssd_kernel(tc, kT, qT, dk, t, v, S, dq, out_0, out_1, out_2):
    nc = tc.nc
    with ExitStack() as ctx:
        sb = ctx.enter_context(tc.tile_pool(name="sb", bufs=1))
        ps = ctx.enter_context(tc.psum_pool(name="ps", bufs=1))
        ctx.enter_context(tc.manual_schedule())

        def tiles(name, shape, dtype):
            return [sb.tile(shape, dtype, name="%s%d" % (name, s), align_bytes=64) for s in range(SETS)]

        raw = {n: tiles(n + "_raw", [P, PACK, W], F32) for n in ("k", "q", "S", "v")}
        dk_sb = tiles("dk_sb", [P, SIDE, W], F32)
        grouped = {n: tiles(n + "_grp", [P, W, PACK], BF16) for n in ("k", "q", "v", "S", "p", "o")}
        codes = {n: tiles(n + "_codes", [P, W], U32) for n in ("k", "q", "v", "S", "p", "o")}
        scales = {n: tiles(n + "_scales", [P, W], U8) for n in ("k", "q", "v", "S", "p")}
        o_scales = sb.tile([P, SETS, W], U8, name="o_scales", align_bytes=64)
        scales["o"] = [o_scales[:, s, :] for s in range(SETS)]
        p_nat = tiles("p_nat", [P, SIDE, W], BF16)
        p_row = tiles("p_row", [P, PACK, W], BF16)
        o_nat = tiles("o_nat", [P, SIDE, W], F32)
        ob_nat = tiles("ob_nat", [P, SIDE, W], BF16)
        o_row = tiles("o_row", [P, PACK, W], BF16)
        ys_sb = tiles("ys_sb", [P, SIDE, W], F32)
        stage = sb.tile([P, ROWS], F32, name="stage", align_bytes=64)
        cols = sb.tile([P, ROWS], F32, name="cols", align_bytes=64)
        banks = [[ps.tile([P, 4, W], F32, name="bank%d_%d" % (s, c)) for c in range(SIDE)] for s in range(SETS)]

        def load(queue, name, src, s):
            rows = src.rearrange("g d w -> (g d) w")[s * P * PACK : (s + 1) * P * PACK, :]
            queue.dma_start(out=raw[name][s][:], in_=rows.rearrange("(p j) w -> p j w", j=PACK))

        def load_dk(queue, s):
            queue.dma_start(out=dk_sb[s][:], in_=dk[s * SIDE : (s + 1) * SIDE].rearrange("c i q -> i c q"))

        def interleave(copy, dst, src, lo=0, hi=W):
            copy(
                out=dst[:, lo:hi, :].rearrange("p (c i) j -> p c j i", i=4),
                in_=src[:, :, lo:hi].rearrange("p j (c i) -> p c j i", i=4),
            )

        def shared(dst, src, cut):
            interleave(nc.vector.tensor_copy, dst, src, 0, cut)
            interleave(nc.scalar.copy, dst, src, cut, W)

        def quantise(name, s):
            nc.vector.quantize_mx(
                out=codes[name][s][:].bitcast(FP8X4),
                scales=scales[name][s][:, :],
                in_=grouped[name][s][:].rearrange("p w j -> p (w j)"),
            )

        def product(slot, a, b, s):
            for c in range(SIDE):
                r = slice(c * ROWS, (c + 1) * ROWS)
                nc.tensor.matmul_mx(
                    out=banks[s][c][:, slot, :],
                    lhsT=codes[a][s][r, :].bitcast(FP8X4),
                    lhsT_scale=scales[a][s][r, :],
                    rhs=codes[b][s][r, :].bitcast(FP8X4),
                    rhs_scale=scales[b][s][r, :],
                    start=True,
                    stop=True,
                )

        def column(which, g):
            j = 4 * g + which
            return cols[:, j : j + 1]

        def weights(s, order=range(SIDE)):
            for c in order:
                nc.vector.scalar_tensor_tensor(
                    out=p_nat[s][:, c, :], in0=banks[s][c][:, 0, :], scalar=column(0, s * SIDE + c),
                    in1=dk_sb[s][:, c, :], op0=ALU.mult, op1=ALU.mult,
                )
                nc.sync.dma_start(out=p_row[s][c * ROWS : (c + 1) * ROWS, :, :], in_=p_nat[s][:, c, :])

        def state_part(s):
            for c in range(SIDE):
                nc.scalar.activation(
                    out=ys_sb[s][:, c, :], in_=banks[s][c][:, 1, :], func=ACT.Copy, scale=column(1, s * SIDE + c)
                )

        def regroup_result(s, c, queue):
            queue.dma_start(out=o_row[s][c * ROWS : (c + 1) * ROWS, :, :], in_=ob_nat[s][:, c, :])

        def result(s, dst, order=range(SIDE)):
            for c in order:
                nc.vector.tensor_tensor(
                    out=dst[s][:, c, :], in0=banks[s][c][:, 2, :], in1=ys_sb[s][:, c, :], op=ALU.add
                )
                if dst is ob_nat:
                    regroup_result(s, c, nc.sync if c < 2 else nc.scalar)

        def store_result(s, queue=nc.scalar, lo=0, hi=SIDE):
            rows = out_0[(s * SIDE + lo) * Q : (s * SIDE + hi) * Q, :]
            queue.dma_start(out=rows.rearrange("(c q) e -> q c e", q=Q), in_=o_nat[s][:, lo:hi, :])

        def store_words(s):
            nc.sync.dma_start(
                out=out_1[s].rearrange("x e u -> x (e u)").bitcast(I32), in_=codes["o"][s][:].bitcast(I32)
            )

        def store_scales():
            scale_rows = out_2.bitcast(I32)
            for c in range(SIDE):
                queue = nc.scalar if c % 2 == 0 else nc.sync
                queue.dma_start(
                    out=scale_rows[:, 4 * c : 4 * c + 4, :].rearrange("s f e -> f s e"),
                    in_=o_scales[c * ROWS : c * ROWS + 4, :, :].bitcast(I32),
                )

        vcopy = nc.vector.tensor_copy
        scopy = nc.scalar.copy

        nc.vector.memset(stage[:], 0.0)
        load(nc.sync, "k", kT, 0)
        load(nc.sync, "q", qT, 0)
        for which, src in enumerate((t, dq)):
            nc.sync.dma_start(out=stage[which:P:4, :], in_=src.rearrange("g (a r) o -> a g (r o)", a=P // ROWS))
        load(nc.sync, "k", kT, 1)
        load(nc.sync, "q", qT, 1)
        for s in range(SETS):
            load_dk(nc.sync, s)
        load(nc.sync, "S", S, 0)
        load(nc.sync, "S", S, 1)
        load(nc.sync, "v", v, 0)

        interleave(scopy, grouped["k"][0], raw["k"][0])
        interleave(vcopy, grouped["q"][0], raw["q"][0])
        quantise("k", 0)
        quantise("q", 0)
        product(0, "k", "q", 0)
        nc.vector.transpose(out=cols[:], in_=stage[:])
        interleave(scopy, grouped["k"][1], raw["k"][1])
        interleave(vcopy, grouped["q"][1], raw["q"][1])
        quantise("k", 1)
        quantise("q", 1)
        product(0, "k", "q", 1)
        weights(0, ORDER)
        load(nc.sync, "v", v, 1)
        weights(1, ORDER)
        interleave(vcopy, grouped["S"][0], raw["S"][0])
        interleave(scopy, grouped["S"][1], raw["S"][1])
        quantise("S", 0)
        product(1, "q", "S", 0)
        state_part(0)
        interleave(vcopy, grouped["v"][0], raw["v"][0])
        quantise("S", 1)
        product(1, "q", "S", 1)
        state_part(1)
        quantise("v", 0)
        interleave(vcopy, grouped["p"][0], p_row[0])
        quantise("p", 0)
        product(2, "p", "v", 0)
        interleave(vcopy, grouped["v"][1], raw["v"][1])
        interleave(vcopy, grouped["p"][1], p_row[1])
        quantise("v", 1)
        quantise("p", 1)
        product(2, "p", "v", 1)
        result(0, ob_nat, ORDER[:1])
        result(0, ob_nat, ORDER[1:])
        result(1, ob_nat, ORDER)
        result(0, o_nat, ORDER)
        store_result(0, nc.sync)
        interleave(scopy, grouped["o"][0], o_row[0])
        result(1, o_nat, ORDER)
        store_result(1, nc.sync)
        shared(grouped["o"][1], o_row[1], 88)
        for s in range(SETS):
            quantise("o", s)
            store_words(s)
        store_scales()
